import numpy as np, ml_dtypes
CORES = [31,71,111]
N = 3
F = 512
def setup_inputs(rng):
    m = (rng.standard_normal((N, 128, 128), dtype=np.float32) / 11).astype(ml_dtypes.bfloat16)
    return {"m": m, "mt": m.transpose(0, 2, 1).copy(), "x": rng.standard_normal((N, 128, F), dtype=np.float32).astype(ml_dtypes.bfloat16)}
def setup_inputs_big(rng):
    d = setup_inputs(rng)
    for k in ("x",): d[k] = (d[k].astype(np.float32) * 1048576.0).astype(d[k].dtype)
    return d
def setup_inputs_small(rng):
    d = setup_inputs(rng)
    for k in ("x",): d[k] = (d[k].astype(np.float32) * (1 / 1048576.0)).astype(d[k].dtype)
    return d
def setup_inputs_apart(rng):
    d = setup_inputs(rng)
    f = (10.0 ** rng.permutation(np.linspace(-1.5, 1.5, N))).astype(np.float32).reshape(N, 1, 1)
    for k in ("x",): d[k] = (d[k].astype(np.float32) * f).astype(d[k].dtype)
    return d
def reference(m, mt, x):
    M, X = m.astype(np.float64), x.astype(np.float64)
    y = np.zeros((N, 128, F)); p = X[0]
    for r in range(N):
        p = M[r].T @ p
        y[r] = p
    return {"y": y.astype(ml_dtypes.bfloat16)}

@@ -1,0 +1,101 @@
+from concourse.bass import DstId, RemoteDMATransfer
+
+F = 512
+H = F // 2
+
+SCRATCH = {
+    "xs": ("sbuf", [128, F], "bfloat16"),
+    "ms": ("sbuf", [128, 128], "bfloat16"),
+    "mts": ("sbuf", [128, 128], "bfloat16"),
+    "mtl": ("sbuf", [128, 128], "bfloat16"),
+    "cs": ("sbuf", [128, 128], "bfloat16"),
+    "pin": ("sbuf", [128, F], "bfloat16"),
+    "ps": ("sbuf", [128, F], "bfloat16"),
+    "acca": ("psum", [128, 512], "float32"),
+    "accb": ("psum", [128, 512], "float32"),
+    "accc": ("psum", [128, 512], "float32"),
+}
+SEMAPHORES = ["ld", "ldt", "mma", "mmb", "mmc", "cp", "cpc", "arrp", "arrm", "sent", "st"]
+
+
+def _bits(mask):
+    return [b for b in range(16) if (mask >> b) & 1]
+
+
+def _mask_of(bits):
+    m = 0
+    for b in bits:
+        m |= 1 << b
+    return m
+
+
+def _product(g, T, lhsT, rhs):
+    s = T.sem
+    g.tensor.matmul(T.acca[:, 0:H], lhsT, rhs[:, 0:H], start=True, stop=True).then_inc(s.mma, 1)
+    g.tensor.matmul(T.accb[:, 0:H], lhsT, rhs[:, H:F], start=True, stop=True).then_inc(s.mmb, 1)
+    g.vector.wait_ge(s.mma, 1)
+    g.vector.tensor_copy(T.ps[:, 0:H], T.acca[:, 0:H]).then_inc(s.cp, 1)
+    g.vector.wait_ge(s.mmb, 1)
+    g.vector.tensor_copy(T.ps[:, H:F], T.accb[:, 0:H]).then_inc(s.cp, 1)
+
+
+def rank_program(g, core, T, topo):
+    rank = T.rank_of(core)
+    if rank is None:
+        return
+    s = T.sem
+    r0, r1, r2 = T.cores
+
+    if rank == 0:
+        g.sync.dma_start(T.xs[:], T.x[:]).then_inc(s.ld, 16)
+        g.scalar.dma_start(T.ms[:], T.m[:]).then_inc(s.ld, 16)
+        g.tensor.wait_ge(s.ld, 32)
+        _product(g, T, T.ms[:], T.xs)
+        assert topo.may_write(core, r1) and topo.may_write(core, r2)
+        bits = _bits(topo.mask(core, r1) & topo.mask(core, r2))
+        half = len(bits) // 2
+        tr = []
+        for dst, eb in ((r1, bits[:half]), (r2, bits[half:])):
+            rid, pid, _ = topo.addr(dst)
+            tr.append(RemoteDMATransfer(dst_ids=[DstId(rid=rid, pnc=pid)], dma_engine_mask=_mask_of(eb),
+                                        remote_sem=s.arrp, src=T.ps[:], dst=T.pin[:]))
+        g.wait_ge(s.cp, 2)
+        g.remote_dma_fused(tr, local_sem=s.sent)
+        g.sync.wait_ge(s.cp, 2)
+        g.sync.wait_ge(s.sent, len(bits))
+        g.sync.dma_start(T.y[:], T.ps[:]).then_inc(s.st, 16)
+        g.sync.wait_ge(s.st, 16)
+        return
+
+    n_arr = len(_bits(topo.mask(r0, r1) & topo.mask(r0, r2))) // 2
+
+    if rank == 1:
+        g.sync.dma_start(T.mts[:], T.mt[:]).then_inc(s.ldt, 16)
+        g.scalar.dma_start(T.ms[:], T.m[:]).then_inc(s.ld, 16)
+        assert topo.may_write(core, r2)
+        mk = topo.mask(core, r2)
+        rid, pid, _ = topo.addr(r2)
+        g.wait_ge(s.ldt, 16)
+        g.remote_dma(T.mtl[:], T.mts[:], remote_sem=s.arrm, local_sem=s.sent, pid=pid, routing_id=rid,
+                     dma_engine_mask=mk)
+        g.tensor.wait_ge(s.ld, 16)
+        g.tensor.wait_ge(s.arrp, n_arr)
+        _product(g, T, T.ms[:], T.pin)
+        g.sync.wait_ge(s.cp, 2)
+        g.sync.dma_start(T.y[:], T.ps[:]).then_inc(s.st, 16)
+        g.sync.wait_ge(s.st, 16)
+        g.wait_ge(s.sent, len(_bits(mk)))
+        return
+
+    g.sync.dma_start(T.ms[:], T.m[:]).then_inc(s.ld, 16)
+    g.tensor.wait_ge(s.ld, 16)
+    g.tensor.wait_ge(s.arrm, len(_bits(topo.mask(r1, core))))
+    g.tensor.matmul(T.accc[:, 0:128], T.mtl[:], T.ms[:], start=True, stop=True).then_inc(s.mmc, 1)
+    g.vector.wait_ge(s.mmc, 1)
+    g.vector.tensor_copy(T.cs[:], T.accc[:, 0:128]).then_inc(s.cpc, 1)
+    g.tensor.wait_ge(s.cpc, 1)
+    g.tensor.wait_ge(s.arrp, n_arr)
+    _product(g, T, T.cs[:], T.pin)
+    g.sync.wait_ge(s.cp, 2)
+    g.sync.dma_start(T.y[:], T.ps[:]).then_inc(s.st, 16)
+    g.sync.wait_ge(s.st, 16)

@@ -1,5 +1,3 @@
-from concourse.bass import DstId, RemoteDMATransfer
-
 F = 512
 H = F // 2
 
@@ -15,7 +13,7 @@ SCRATCH = {
     "accb": ("psum", [128, 512], "float32"),
     "accc": ("psum", [128, 512], "float32"),
 }
-SEMAPHORES = ["ld", "ldt", "mma", "mmb", "mmc", "cp", "cpc", "arrp", "arrm", "sent", "st"]
+SEMAPHORES = ["ld", "ldt", "ldx", "mma", "mmb", "mmc", "cp", "cpc", "arrp", "arrm", "sent", "st"]
 
 
 def _bits(mask):
@@ -39,62 +37,60 @@ def _product(g, T, lhsT, rhs):
     g.vector.tensor_copy(T.ps[:, H:F], T.accb[:, 0:H]).then_inc(s.cp, 1)
 
 
+def _send(g, T, topo, dst, out, in_, sem, bits):
+    rid, pid, _ = topo.addr(dst)
+    g.remote_dma(out, in_, remote_sem=sem, local_sem=T.sem.sent, pid=pid, routing_id=rid,
+                 dma_engine_mask=_mask_of(bits))
+
+
 def rank_program(g, core, T, topo):
     rank = T.rank_of(core)
     if rank is None:
         return
     s = T.sem
     r0, r1, r2 = T.cores
+    bits0 = _bits(topo.mask(r0, r1) & topo.mask(r0, r2))
+    ea, eb = bits0[0::2], bits0[1::2]
 
     if rank == 0:
-        g.sync.dma_start(T.xs[:], T.x[:]).then_inc(s.ld, 16)
-        g.scalar.dma_start(T.ms[:], T.m[:]).then_inc(s.ld, 16)
-        g.tensor.wait_ge(s.ld, 32)
-        _product(g, T, T.ms[:], T.xs)
         assert topo.may_write(core, r1) and topo.may_write(core, r2)
-        bits = _bits(topo.mask(core, r1) & topo.mask(core, r2))
-        half = len(bits) // 2
-        tr = []
-        for dst, eb in ((r1, bits[:half]), (r2, bits[half:])):
-            rid, pid, _ = topo.addr(dst)
-            tr.append(RemoteDMATransfer(dst_ids=[DstId(rid=rid, pnc=pid)], dma_engine_mask=_mask_of(eb),
-                                        remote_sem=s.arrp, src=T.ps[:], dst=T.pin[:]))
+        g.scalar.dma_start(T.mts[:], T.mt[:]).then_inc(s.ldt, 16)
+        g.sync.dma_start(T.xs[:], T.x[:]).then_inc(s.ldx, 16)
+        g.scalar.dma_start(T.ms[:], T.m[:]).then_inc(s.ld, 16)
+        g.wait_ge(s.ldt, 16)
+        _send(g, T, topo, r1, T.mtl[:], T.mts[:], s.arrm, eb)
+        g.wait_ge(s.ldx, 16)
+        _send(g, T, topo, r1, T.pin[:], T.xs[:], s.arrp, ea)
+        g.tensor.wait_ge(s.ldx, 16)
+        g.tensor.wait_ge(s.ld, 16)
+        _product(g, T, T.ms[:], T.xs)
         g.wait_ge(s.cp, 2)
-        g.remote_dma_fused(tr, local_sem=s.sent)
+        _send(g, T, topo, r2, T.pin[:], T.ps[:], s.arrp, eb)
         g.sync.wait_ge(s.cp, 2)
-        g.sync.wait_ge(s.sent, len(bits))
+        g.sync.wait_ge(s.sent, len(ea) + 2 * len(eb))
         g.sync.dma_start(T.y[:], T.ps[:]).then_inc(s.st, 16)
         g.sync.wait_ge(s.st, 16)
         return
-
-    n_arr = len(_bits(topo.mask(r0, r1) & topo.mask(r0, r2))) // 2
 
     if rank == 1:
+        assert topo.may_write(core, r2)
+        mk = _bits(topo.mask(core, r2))
         g.sync.dma_start(T.mts[:], T.mt[:]).then_inc(s.ldt, 16)
         g.scalar.dma_start(T.ms[:], T.m[:]).then_inc(s.ld, 16)
-        assert topo.may_write(core, r2)
-        mk = topo.mask(core, r2)
-        rid, pid, _ = topo.addr(r2)
         g.wait_ge(s.ldt, 16)
-        g.remote_dma(T.mtl[:], T.mts[:], remote_sem=s.arrm, local_sem=s.sent, pid=pid, routing_id=rid,
-                     dma_engine_mask=mk)
-        g.tensor.wait_ge(s.ld, 16)
-        g.tensor.wait_ge(s.arrp, n_arr)
-        _product(g, T, T.ms[:], T.pin)
-        g.sync.wait_ge(s.cp, 2)
-        g.sync.dma_start(T.y[:], T.ps[:]).then_inc(s.st, 16)
-        g.sync.wait_ge(s.st, 16)
-        g.wait_ge(s.sent, len(_bits(mk)))
-        return
-
-    g.sync.dma_start(T.ms[:], T.m[:]).then_inc(s.ld, 16)
+        _send(g, T, topo, r2, T.mtl[:], T.mts[:], s.arrm, mk)
+        g.wait_ge(s.sent, len(mk))
+        n_m, n_p = len(eb), len(ea)
+    else:
+        g.sync.dma_start(T.ms[:], T.m[:]).then_inc(s.ld, 16)
+        n_m, n_p = len(_bits(topo.mask(r1, core))), len(eb)
     g.tensor.wait_ge(s.ld, 16)
-    g.tensor.wait_ge(s.arrm, len(_bits(topo.mask(r1, core))))
+    g.tensor.wait_ge(s.arrm, n_m)
     g.tensor.matmul(T.accc[:, 0:128], T.mtl[:], T.ms[:], start=True, stop=True).then_inc(s.mmc, 1)
     g.vector.wait_ge(s.mmc, 1)
     g.vector.tensor_copy(T.cs[:], T.accc[:, 0:128]).then_inc(s.cpc, 1)
     g.tensor.wait_ge(s.cpc, 1)
-    g.tensor.wait_ge(s.arrp, n_arr)
+    g.tensor.wait_ge(s.arrp, n_p)
     _product(g, T, T.cs[:], T.pin)
     g.sync.wait_ge(s.cp, 2)
     g.sync.dma_start(T.y[:], T.ps[:]).then_inc(s.st, 16)

F = 512
H = F // 2

SCRATCH = {
    "xs": ("sbuf", [128, F], "bfloat16"),
    "ms": ("sbuf", [128, 128], "bfloat16"),
    "mts": ("sbuf", [128, 128], "bfloat16"),
    "mtl": ("sbuf", [128, 128], "bfloat16"),
    "cs": ("sbuf", [128, 128], "bfloat16"),
    "pin": ("sbuf", [128, F], "bfloat16"),
    "ps": ("sbuf", [128, F], "bfloat16"),
    "acca": ("psum", [128, 512], "float32"),
    "accb": ("psum", [128, 512], "float32"),
    "accc": ("psum", [128, 512], "float32"),
}
SEMAPHORES = ["ld", "ldt", "ldx", "mma", "mmb", "mmc", "cp", "cpc", "arrp", "arrm", "sent", "st"]


def _bits(mask):
    return [b for b in range(16) if (mask >> b) & 1]


def _mask_of(bits):
    m = 0
    for b in bits:
        m |= 1 << b
    return m


def _product(g, T, lhsT, rhs):
    s = T.sem
    g.tensor.matmul(T.acca[:, 0:H], lhsT, rhs[:, 0:H], start=True, stop=True).then_inc(s.mma, 1)
    g.tensor.matmul(T.accb[:, 0:H], lhsT, rhs[:, H:F], start=True, stop=True).then_inc(s.mmb, 1)
    g.vector.wait_ge(s.mma, 1)
    g.vector.tensor_copy(T.ps[:, 0:H], T.acca[:, 0:H]).then_inc(s.cp, 1)
    g.vector.wait_ge(s.mmb, 1)
    g.vector.tensor_copy(T.ps[:, H:F], T.accb[:, 0:H]).then_inc(s.cp, 1)


def _send(g, T, topo, dst, out, in_, sem, bits):
    rid, pid, _ = topo.addr(dst)
    g.remote_dma(out, in_, remote_sem=sem, local_sem=T.sem.sent, pid=pid, routing_id=rid,
                 dma_engine_mask=_mask_of(bits))


def rank_program(g, core, T, topo):
    rank = T.rank_of(core)
    if rank is None:
        return
    s = T.sem
    r0, r1, r2 = T.cores
    bits0 = _bits(topo.mask(r0, r1) & topo.mask(r0, r2))
    ea, eb = bits0[0::2], bits0[1::2]

    if rank == 0:
        assert topo.may_write(core, r1) and topo.may_write(core, r2)
        g.scalar.dma_start(T.mts[:], T.mt[:]).then_inc(s.ldt, 16)
        g.sync.dma_start(T.xs[:], T.x[:]).then_inc(s.ldx, 16)
        g.scalar.dma_start(T.ms[:], T.m[:]).then_inc(s.ld, 16)
        g.wait_ge(s.ldt, 16)
        _send(g, T, topo, r1, T.mtl[:], T.mts[:], s.arrm, eb)
        g.wait_ge(s.ldx, 16)
        _send(g, T, topo, r1, T.pin[:], T.xs[:], s.arrp, ea)
        g.tensor.wait_ge(s.ldx, 16)
        g.tensor.wait_ge(s.ld, 16)
        _product(g, T, T.ms[:], T.xs)
        g.wait_ge(s.cp, 2)
        _send(g, T, topo, r2, T.pin[:], T.ps[:], s.arrp, eb)
        g.sync.wait_ge(s.cp, 2)
        g.sync.wait_ge(s.sent, len(ea) + 2 * len(eb))
        g.sync.dma_start(T.y[:], T.ps[:]).then_inc(s.st, 16)
        g.sync.wait_ge(s.st, 16)
        return

    if rank == 1:
        assert topo.may_write(core, r2)
        mk = _bits(topo.mask(core, r2))
        g.sync.dma_start(T.mts[:], T.mt[:]).then_inc(s.ldt, 16)
        g.scalar.dma_start(T.ms[:], T.m[:]).then_inc(s.ld, 16)
        g.wait_ge(s.ldt, 16)
        _send(g, T, topo, r2, T.mtl[:], T.mts[:], s.arrm, mk)
        g.wait_ge(s.sent, len(mk))
        n_m, n_p = len(eb), len(ea)
    else:
        g.sync.dma_start(T.ms[:], T.m[:]).then_inc(s.ld, 16)
        n_m, n_p = len(_bits(topo.mask(r1, core))), len(eb)
    g.tensor.wait_ge(s.ld, 16)
    g.tensor.wait_ge(s.arrm, n_m)
    g.tensor.matmul(T.accc[:, 0:128], T.mtl[:], T.ms[:], start=True, stop=True).then_inc(s.mmc, 1)
    g.vector.wait_ge(s.mmc, 1)
    g.vector.tensor_copy(T.cs[:], T.accc[:, 0:128]).then_inc(s.cpc, 1)
    g.tensor.wait_ge(s.cpc, 1)
    g.tensor.wait_ge(s.arrp, n_p)
    _product(g, T, T.cs[:], T.pin)
    g.sync.wait_ge(s.cp, 2)
    g.sync.dma_start(T.y[:], T.ps[:]).then_inc(s.st, 16)
    g.sync.wait_ge(s.st, 16)
